import numpy as np, ml_dtypes
CORES = [66,74,82,90,194,202,210,218]
N = 8
import mx_ref
BF = ml_dtypes.bfloat16
def gentries(a):
    return np.ascontiguousarray(a.reshape(8, 16, -1).transpose(0, 2, 1)).reshape(8, -1)
def gtable(e):
    e = np.asarray(e); return np.ascontiguousarray(e.reshape(8, -1, 16).transpose(0, 2, 1)).reshape(128, -1).astype(np.int32)
def gcols(t, e):
    v = np.concatenate([t.reshape(8, 16, -1, 4), np.zeros((8, 16, 1, 4), BF)], axis=2)
    return np.ascontiguousarray(np.stack([v[g][:, e[g]] for g in range(8)])).reshape(128, -1)
def tile(rs):
    return np.stack(rs, axis=2).reshape(128, -1).astype(BF)
def pick(q, e):
    c = np.concatenate([q[0].reshape(128, -1, 4), np.zeros((128, 1, 4), np.uint8)], axis=1); s = np.concatenate([q[1], np.ones((16, 1), np.uint8)], axis=1)
    return (np.ascontiguousarray(c[:, e].reshape(128, -1)), np.ascontiguousarray(s[:, e]))
def join(*qs):
    return (np.concatenate([q[0] for q in qs], axis=1), np.concatenate([q[1] for q in qs], axis=1))
def put(q, e, v):
    c, s = q[0].reshape(128, -1, 4).copy(), q[1].copy(); c[:, e] = v[0].reshape(128, -1, 4); s[:, e] = v[1]
    return (c.reshape(128, -1), s)
def pk(c, s):
    return (np.ascontiguousarray(c), mx_ref.live(s))
def emit(q):
    return q[0], q[1]
def packed(v, rng):
    q = [mx_ref.quantize(np.ascontiguousarray(v[r])) for r in range(N)]
    return np.stack([a for a, b in q]), np.stack([mx_ref.plane(b, rng) for a, b in q])
def values_of_codes():
    e, c = np.zeros((128, 128, 4), np.float32), np.zeros((128, 2, 4), np.uint8)
    e[np.arange(128), np.arange(128), 0] = 1
    c[:127, :, 0] = np.arange(256).reshape(2, 128).T[:127]
    return mx_ref.matmul(mx_ref.quantize(e.reshape(128, 512).astype(BF)), (c.reshape(128, 8), np.full((16, 2), 127, np.uint8))).T.reshape(-1).astype(np.float64)
CODE_VALUE, SCALE_VALUE = values_of_codes(), 2.0 ** (np.arange(256) - 127.0)
def decode(q):
    return (CODE_VALUE[q[0]].reshape(16, 8, -1, 4) * SCALE_VALUE[q[1]][:, None, :, None] + 0.0).reshape(128, -1).astype(np.float32)
def f(rng, *shape):
    return mx_ref.flush((rng.standard_normal(shape, dtype=np.float32) * np.exp2(rng.integers(-2, 3, shape[:-1] + (1,)))).astype(BF))
def wide(rng, *shape, cols=0):
    v = rng.standard_normal(shape, dtype=np.float32) * np.exp2(rng.integers(-12, 13, shape)).astype(np.float32)
    if cols: v *= np.repeat(np.exp2(rng.integers(-cols, cols + 1, shape[:-2] + (1, shape[-1] // 4))) * (rng.random(shape[:-2] + (1, shape[-1] // 4)) > 0.0625), 4, axis=-1).astype(np.float32)
    return mx_ref.flush(v.astype(BF))
C, K, R = 288, 144, 3
def big(v):
    v = v.astype(np.float32)
    v[np.abs(v) < np.float32(2.0 ** -16)] = 0
    return v.astype(BF)
def numbers_of(rng):
    return {"x": np.array(f(rng, N, 128, 4 * C)), "u": np.array(f(rng, N, 128, 512)), "v": np.array(f(rng, N, 128, 512))}
def bindings(rng):
    return np.stack([gtable(np.argsort(rng.random((8, C)), axis=1)) for r in range(N)])
def targets(rng):
    return np.stack([gtable(rng.integers(0, C, (8, C))) for r in range(N)])
def layers(rng):
    return np.clip(f(rng, N, 128, 2048).astype(np.float32), -1.75, 1.75).astype(BF).reshape(N, 8, 16, 4, 8, 16, 4)
def planted(rng, quiet, pairs):
    w = layers(rng)
    w[:, :, :, :, :, quiet] = 0
    for a, b in pairs:
        for g in range(8): w[:, g, a, 0, g, b, 0] = 1
    return w
def weights(rng, w):
    c, p = packed(np.ascontiguousarray(w).reshape(N, 128, 2048), rng)
    return {"wc": c, "ws": p}
def setup_inputs(rng):
    return {**numbers_of(rng), "bd": bindings(rng), "ds": targets(rng), **weights(rng, layers(rng))}
def setup_inputs_ties(rng):
    d = numbers_of(rng)
    x = d["x"].reshape(N, 8, 16, C, 4)
    x[:, :, 0] = 0
    x[:, :, 0, :, 0] = rng.integers(-1, 2, (N, 8, C)).astype(np.float32).astype(BF)
    u = d["u"].reshape(N, 128, 128, 4)
    u[:, :, ::16] = 0
    o = rng.permutation(N)
    for r in range(N):
        for h in range(0, 128, 16): u[r, h + 1, h, 0] = 0.0 if r == o[0] else -1.0 if r == o[1] else 1.0
    return {"x": x.reshape(N, 128, 4 * C), "u": u.reshape(N, 128, 512), "v": d["v"], "bd": bindings(rng), "ds": targets(rng), **weights(rng, planted(rng, [0, 1], [(0, 1)]))}
def setup_inputs_near(rng):
    d = numbers_of(rng)
    x = d["x"].astype(np.float32).reshape(N, 8, 16, C, 4)
    x[:, :, :6] = 0
    x[:, :, 8:] = 0
    x[:, :, 0, :, 0] = 1
    x[:, :, 1, :, 0] = 1
    x[:, :, 4, :, 0] = rng.integers(-8, 9, (N, 8, C)) * 0.125
    x[:, :, 8, :, 0] = rng.integers(-8, 9, (N, 8, C)) * 2.0 ** -17
    u = d["u"].reshape(N, 128, 128, 4)
    u[:, :, ::16] = 0
    o = rng.permutation(N) % 4
    for r in range(N):
        c = np.where(rng.permutation(8) < 2, 1.0, -1.0)
        k = 1.0 if o[r] == 0 else 2.0 ** -12
        for h in range(0, 128, 16):
            if o[r] < 2:
                u[r, h + 2, h, 0] = c[h // 16] * k
                u[r, h + 3, h, 0] = c[h // 16] * k * 2.0 ** -10
                u[r, h + 10, h, 0] = k * 2.0 ** -4
            elif o[r] == 2:
                u[r, h + 10, h, 0] = 1.125 * 2.0 ** -30
                u[r, h + 11, h, 0] = -2.0 ** -30
            else:
                u[r, h + 5, h, 0] = 1.0
                u[r, h + 10, h, 0] = 1.0
    w = planted(rng, [0, 1, 2, 3, 4, 5, 8, 9, 10, 11, 12, 13, 14, 15], [(0, 2), (1, 3), (4, 5), (8, 10), (8, 11)])
    return {"x": x.reshape(N, 128, 4 * C).astype(BF), "u": u.reshape(N, 128, 512), "v": d["v"], "bd": bindings(rng), "ds": targets(rng), **weights(rng, w)}
def setup_inputs_ends(rng):
    d = numbers_of(rng)
    o = (np.arange(N) + rng.integers(N)) % N
    few = N // 4
    x = 2.0 ** 20 * (1 - 0.125 * rng.integers(0, 2, (N, 1, C, 1))) * np.ones((1, 128, 1, 4))
    c = 2.0 ** -30 * rng.choice([-1.0, 1.0], (128, 1, 4))
    less = rng.permutation(8) % 2 == 0
    u = d["u"].reshape(N, 128, 128, 4)
    v = rng.choice([-1.0, 1.0], (N, 128, 512))
    w = np.where(rng.random((N, 128, 512, 4)) < rng.random((N, 1, 512, 1)), 1.5, 1.75).reshape(N, 128, 2048)
    e, t = bindings(rng), np.zeros((N, 8, C), int)
    e[o[0]] = gtable(np.stack([np.arange(C)[::-1]] * 8))
    e[o[few]] = gtable(np.stack([np.arange(C)] * 8))
    for i in range(N):
        r = o[i]
        v[r] *= 2.0 ** 30 if i % 2 == 1 else 2.0 ** -30
        s = np.full(8, -1.0)
        if i == few:
            s = np.where(less, -1.0, 1.0)
            t[r][~np.roll(less, 1)] = C - 1
        u[r, :, ::16] = (s * (2.0 ** -30 if i < few else 2.0 ** 30)).astype(np.float32).astype(BF)[None, :, None]
        if i < few:
            x[r] = c
            t[r] = C - 1
            w[o[i + 1]] = 0
    return {"x": x.astype(np.float32).reshape(N, 128, 4 * C).astype(BF), "u": u.reshape(N, 128, 512), "v": v.astype(np.float32).astype(BF), "bd": e, "ds": np.stack([gtable(t[r]) for r in range(N)]), **weights(rng, w.astype(np.float32).astype(BF))}
def setup_inputs_odd(rng):
    d = numbers_of(rng)
    n = (N, 8, 16, C, 4)
    x = (1 + (2 * rng.integers(0, 64, n) + 1) * 2.0 ** -7) * np.exp2(-rng.integers(8, 15, n).astype(np.float64)) * rng.choice([-1.0, 1.0], n)
    x[:, :, ::8, :, 0] = rng.choice([1.96875, 1.875], (N, 8, 2, C))
    x[:, :, 9, :, 0] = 1.875
    x[:, :, 10, :, 0] = 0.09375
    x[:, :, 11, :, 0] = rng.integers(-15, 16, (N, 8, C)) * 0.125
    u = d["u"].reshape(N, 128, 128, 4)
    u[:, :, ::16] = 0
    for h in range(0, 128, 16): u[:, h + 13, h, 0] = 1.0
    w = planted(rng, [8, 9, 10, 11, 12, 13, 14, 15], [(9, 12), (10, 12), (11, 13)])
    for g in range(8): w[:, g, 11, 0, g, 13, 0] = 2.0 ** -12
    return {"x": x.astype(np.float32).reshape(N, 128, 4 * C).astype(BF), "u": u.reshape(N, 128, 512), "v": d["v"], "bd": bindings(rng), "ds": targets(rng), **weights(rng, w)}
def setup_inputs_spread(rng):
    d = setup_inputs(rng)
    d["x"] = big(wide(rng, N, 128, 4 * C, cols=4))
    return d
def check_inputs(d):
    b = []
    for k, m in (("x", 20), ("u", 30), ("v", 30)):
        a = np.abs(d[k].astype(np.float32))
        if not (np.isfinite(a).all() and ((a == 0) | (a >= 2.0 ** -30) & (a <= 2.0 ** m)).all()): b.append("a value of " + k)
    if not ((d["ds"] >= 0) & (d["ds"] < C)).all(): b.append("an entry of ds")
    none, least, most = [emit(mx_ref.quantize(np.full((128, 16), k, np.float32).astype(BF)))[1][0, 0] for k in (0.0, 2.0 ** -30, 1.75)]
    for r in range(N):
        if (np.sort(gentries(d["bd"][r]), axis=1) != np.arange(C)).any(): b.append("bd: not every port once in a group")
        if ((d["wc"][r] == 0x7F) | (d["wc"][r] == 0xFF)).any(): b.append("wc: a code that is no number")
        s = mx_ref.live(d["ws"][r])
        if ((s != none) & ((s < least) | (s > most))).any(): b.append("ws: a scale out of range")
        if (((d["wc"][r].reshape(16, 8, 512, 4) & 0x7F) != 0) & (s == none)[:, None, :, None]).any(): b.append("wc: a number other than zero at the scale of zeros")
        if not (np.abs(decode(pk(d["wc"][r], d["ws"][r]))) <= 1.75).all(): b.append("wc and ws: a number beyond 1.75 in size")
    return b
def reference(x, u, v, bd, ds, wc, ws):
    qu = [mx_ref.quantize(u[r]) for r in range(N)]
    lay = [pk(wc[r], ws[r]) for r in range(N)]
    now = [x[r] for r in range(N)]
    port = np.stack([gentries(bd[r]) for r in range(N)]).astype(np.int64)
    aim = np.stack([gentries(ds[r]) for r in range(N)]).astype(np.int64)
    for step in range(R):
        iv = np.argsort(port, axis=2)
        m = np.take_along_axis(iv, aim, axis=2)
        own = [decode(mx_ref.quantize(now[r])).astype(BF) for r in range(N)]
        z = [((own[r].astype(np.float32) + gcols(own[r], m[r]).astype(np.float32)) * np.float32(0.5)).astype(BF) for r in range(N)]
        out = [mx_ref.quantize(gcols(z[r], iv[r][:, K:])) for r in range(N)]
        reply = []
        for r in range(N):
            met = ((decode(out[(r - 1) % N]) + gcols(own[r], iv[r][:, :K]).astype(np.float32)) * np.float32(0.5)).astype(BF)
            q = mx_ref.quantize(met)
            reply.append(mx_ref.quantize(tile([mx_ref.matmul(pick(lay[r], np.arange(128 * b, 128 * b + 128)), q) * np.float32(0.0078125) for b in range(4)])))
        for r in range(N):
            q = reply[(r + 1) % N]
            back = gcols(decode(q).astype(BF), np.where(port[r] < K, -1, port[r] - K))
            now[r] = (z[r].astype(np.float32) + back.astype(np.float32)).astype(BF)
            s = mx_ref.matmul(qu[r], q)[::16] + np.float32(0.0)
            place = np.argsort(np.argsort(s, axis=1, kind="stable"), axis=1)
            for g in range(8):
                h = (g + 1) % 8
                k = np.nonzero(s[g] <= 0)[0]
                low, high = iv[r, h, place[g, k]], iv[r, h, K + k]
                port[r, h, low] = K + k
                port[r, h, high] = place[g, k]
    y, ob = np.zeros((N, 128, C), np.float32), np.zeros((N, 8, C), np.float32)
    oc, osc = np.zeros((N, 128, 4 * C), np.uint8), np.zeros((N, 16, C), np.uint8)
    for r in range(N):
        q = mx_ref.quantize(now[r])
        y[r] = mx_ref.matmul(mx_ref.quantize(v[r]), q)
        ob[r] = port[r]
        oc[r], osc[r] = emit(q)
    return {"y": y, "ob": ob, "oc": oc, "osc": osc}

from concourse.mybir import dt, AluOpType, AxisListType, ActivationFunctionType

C, K, R = 288, 144, 3
CW = 146
OPT = {"na": (7, 7, 6), "ns": (7, 7, 3), "fpos": (7, 7, 0), "xa": 3, "xb": 22, "ypos": 6, "qpos": (4, 4, 4), "late": (0, 0, 0), "xv": 16}
BIG = 2.0 ** 96
X4, U8 = "float8_e4m3fn_x4", "uint8"

SCRATCH = {
    "xin": ("sbuf", [128, 4 * C], "bfloat16"), "uin": ("sbuf", [128, 512], "bfloat16"), "vin": ("sbuf", [128, 512], "bfloat16"),
    "bdi": ("sbuf", [128, 18], "int32"), "dsi": ("sbuf", [128, 18], "int32"),
    "wq": ("sbuf", [128, 512], X4), "wsc": ("sbuf", [128, 512], U8),
    "qu": ("sbuf", [128, 128], X4), "su": ("sbuf", [128, 128], U8),
    "qu2": ("sbuf", [128, 128], X4), "su2": ("sbuf", [128, 128], U8),
    "qv": ("sbuf", [128, 128], X4), "sv": ("sbuf", [128, 128], U8),
    "half": ("sbuf", [128, 128], "bfloat16"),
    "eb": ("sbuf", [128, 520], "bfloat16"), "eb1": ("sbuf", [128, 520], "bfloat16"),
    "qeh": ("sbuf", [128, 512], X4), "seh": ("sbuf", [128, 512], U8),
    "qe1": ("sbuf", [128, 512], X4), "se1": ("sbuf", [128, 512], U8),
    "qx": ("sbuf", [128, C], X4), "sx": ("sbuf", [128, C], U8),
    "qf": ("sbuf", [128, C], X4), "sf": ("sbuf", [128, C], U8),
    "qw": ("sbuf", [128, K], X4), "sw": ("sbuf", [128, K], U8),
    "qa": ("sbuf", [128, K], X4), "sa": ("sbuf", [128, K], U8),
    "fh": ("sbuf", [128, 4 * C], "bfloat16"), "xs": ("sbuf", [128, 4 * C], "bfloat16"), "xf": ("sbuf", [128, 4 * C], "bfloat16"),
    "g1": ("sbuf", [128, 4 * K], "bfloat16"), "g1l": ("sbuf", [128, 4 * K], "bfloat16"), "xa": ("sbuf", [128, 4 * K], "bfloat16"),
    "mt": ("sbuf", [128, 4 * K], "bfloat16"), "vt": ("sbuf", [128, 4 * K], "bfloat16"), "ht": ("sbuf", [128, 4 * K], "bfloat16"),
    "iof": ("sbuf", [128, C], "float32"), "phif": ("sbuf", [128, C], "float32"),
    "jj16": ("sbuf", [128, K], "float32"), "jj4": ("sbuf", [128, K], "float32"),
    "pidx": ("sbuf", [128, 1], "int32"), "pi3": ("sbuf", [128, 4], "int32"), "pf": ("sbuf", [128, 8], "float32"),
    "n16": ("sbuf", [128, C], "float32"), "rb16": ("sbuf", [128, C], "float32"),
    "n4": ("sbuf", [128, C], "float32"), "rb4": ("sbuf", [128, C], "float32"),
    "n16s": ("sbuf", [128, K], "float32"), "rs16": ("sbuf", [128, K], "bfloat16"), "kw": ("sbuf", [128, 9], "float32"),
    "ivrow": ("sbuf", [128, C], "float32"), "sig": ("sbuf", [128, 3 * 432], "float32"), "urow": ("sbuf", [128, C], "float32"),
    "trow0": ("sbuf", [128, C], "float32"), "trow1": ("sbuf", [128, C], "float32"),
    "e1": ("sbuf", [128, K], "float32"), "e2": ("sbuf", [128, K], "float32"),
    "f1": ("sbuf", [128, C], "float32"), "f2": ("sbuf", [128, C], "float32"),
    "h1": ("sbuf", [128, C], "float32"), "h2": ("sbuf", [128, C], "float32"),
    "k1": ("sbuf", [128, 18], "float32"), "k2": ("sbuf", [128, 18], "float32"),
    "d1": ("sbuf", [128, K], "float32"), "hold": ("sbuf", [128, K], "float32"),
    "eq": ("sbuf", [128, K], "bfloat16"), "eqs": ("sbuf", [128, K], "bfloat16"), "flag": ("sbuf", [128, 9], "float32"),
    "cmp": ("sbuf", [128, 9 * CW], "bfloat16"), "cnt": ("sbuf", [128, 9], "float32"), "af": ("sbuf", [128, 9], "float32"),
    "bdw": ("sbuf", [128, 18], "uint16"), "dsw": ("sbuf", [128, 18], "uint16"), "uoff": ("sbuf", [128, 8], "uint16"),
    "aw": ("sbuf", [128, 40], "uint16"), "alw": ("sbuf", [128, 30], "uint16"), "al4": ("sbuf", [128, 40], "uint16"),
    "bw": ("sbuf", [128, 36], "uint16"), "blw": ("sbuf", [128, 36], "uint16"),
    "tw": ("sbuf", [128, 36], "uint16"), "pw": ("sbuf", [128, 18], "uint16"), "xw": ("sbuf", [128, 72], "uint16"),
    "obr": ("sbuf", [128, C], "float32"), "yb": ("sbuf", [128, C], "float32"),
    "ps": ("psum", [128, 4096], "float32"),
}
for _r in range(R):
    for _n in ("qm", "lm", "qh", "lh"):
        SCRATCH["%s%d" % (_n, _r)] = ("sbuf", [128, K], X4)
        SCRATCH["s%s%d" % (_n, _r)] = ("sbuf", [128, K], U8)

POOL = {"v": 60, "a": 36, "t": 16, "g": 6}
NDMA = 16
SEMAPHORES = (["%s%d" % (q, i) for q in POOL for i in range(POOL[q])] + ["dma%d" % i for i in range(NDMA)]
              + ["am%d" % r for r in range(R)] + ["ah%d" % r for r in range(R)] + ["left"])


def emit(ops, queues, T):
    n = len(ops)
    writer, readers, bank = {}, {}, {}
    known = {q: 0 for q in queues}
    snap, waits, signals = [0] * n, [None] * n, [False] * n
    for i, o in enumerate(ops):
        q = o["q"]
        deps = set()
        for k in o["r"]:
            if k in writer:
                deps.add(writer[k])
        for k in o["w"]:
            if k in writer and o["kind"] != "acc":
                deps.add(writer[k])
            deps.update(readers.get(k, []))
        for k in list(o["r"]) + list(o["w"]):
            if k.startswith("ps"):
                deps.update(j for j in bank.get(k, []) if ops[j]["q"] != q)
        mine = []
        for j in sorted(deps, reverse=True):
            if not known[q] >> j & 1:
                mine.append(j)
                signals[j] = True
                known[q] |= snap[j] | 1 << j
        waits[i], snap[i] = mine, known[q]
        for k in o["r"]:
            readers.setdefault(k, []).append(i)
        for k in o["w"]:
            writer[k], readers[k] = i, []
        for k in list(o["r"]) + list(o["w"]):
            if k.startswith("ps"):
                bank[k] = [j for j in bank.get(k, []) if not known[q] >> j & 1] + [i]
    last, count, mark, ndma, tail = {}, {}, {}, 0, []
    for i, o in enumerate(ops):
        q = o["q"]
        for j in reversed(waits[i]):
            queues[q].wait_ge(T.sem[mark[j][0]], mark[j][1])
        for s, val in o["ext"]:
            queues[q].wait_ge(T.sem[s], val)
        ins = o["f"](*o["a"], **o["k"])
        if o["kind"] == "dma":
            s = "dma%d" % ndma
            ndma += 1
            ins.then_inc(T.sem[s], 16)
            mark[i] = (s, 16)
            if not signals[i]:
                tail.append((q, s))
        elif signals[i]:
            for m in range(POOL[q]):
                s = "%s%d" % (q, m)
                if s not in last or snap[i] >> last[s] & 1:
                    break
            else:
                raise ValueError("out of semaphores on queue " + q)
            last[s], count[s] = i, count.get(s, 0) + 1
            ins.then_inc(T.sem[s], 1)
            mark[i] = (s, count[s])
    for q, s in tail:
        queues[q].wait_ge(T.sem[s], 16)


def rank_program(g, core, T, topo):
    rank = T.rank_of(core)
    if rank is None:
        return
    n = len(T.cores)
    nxt, prv = T.cores[(rank + 1) % n], T.cores[(rank - 1) % n]
    V, A, PE, SY = g.vector, g.scalar, g.tensor, g.sync
    queues = {"g": g, "v": V, "a": A, "t": PE, "s": SY}
    OP, FN = AluOpType, ActivationFunctionType
    ops = []
    sent = [0]

    def op(q, f, a, r, w, k=None, kind="c", ext=()):
        ops.append({"q": q, "f": f, "a": a, "k": k or {}, "r": r, "w": w, "kind": kind, "ext": ext})

    def dma(q, out, in_, r, w):
        op(q, queues[q].dma_start, (out, in_), r, w, kind="dma")

    def cp(out, in_, r, w):
        op("v", V.tensor_copy, (out, in_), r, w)

    def tt(out, a, b, o, r, w):
        op("v", V.tensor_tensor, (out, a, b, o), r, w)

    def ts(out, a, s1, s2, o, r, w):
        op("v", V.tensor_scalar, (out, a, s1, s2) + tuple(o), r, w)

    def act(out, in_, r, w, fn=None, **k):
        op("a", A.activation, (out, in_, fn or FN.Copy), r, w, k)

    def quant(q, s, in_, r, w):
        op("v", V.quantize_mx, (q, s, in_), r, w)

    def hold_scan(out, rb, d, r, w):
        op("v", V.tensor_tensor_scan, (out, rb, d, 0.0, OP.add, OP.min), r, w)

    def bank(b, a=0, e=K):
        return T.ps[:, 512 * b + a:512 * b + e]

    def mm(b, wq, wsc, col, q, s, r, ext=(), start=True, stop=True):
        op("t", PE.matmul_mx, (bank(b), wq[:, col:col + 128], wsc[:, col:col + 128], q, s, start, stop),
           r, ["ps%d" % b], ext=ext, kind="c" if start else "acc")

    def halves(b0, q, s, k, ext=(), start=True, stop=True):
        for b in range(4):
            mm(b0 + b, T.qeh, T.seh, 128 * b, q, s, ["eh%d" % b] + k, ext if b == 0 else (), start, stop)

    def pair_sum(q0, s0, k0, q1, s1, k1, out, keys, both):
        halves(0, q0, s0, [k0], stop=False)
        halves(0, q1, s1, [k1], start=False)
        for b in range(4):
            (cp if both and b % 2 else act)(out[:, b:4 * K:4], bank(b), ["ps%d" % b], [keys[b]])

    def send(name, land, r, dst, sem):
        rid, pid = topo.addr(dst, core)
        mask = topo.mask(core, dst)
        src, to = "%s%d" % (name, r), "%s%d" % (land, r)
        op("g", g.remote_dma, (T[to][:].bitcast(dt.uint8), T[src][:].bitcast(dt.uint8), T.sem[sem], T.sem["left"], pid, rid, mask),
           [src], [], kind="rem")
        op("g", g.remote_dma, (T["s" + to][:], T["s" + src][:], T.sem[sem], T.sem["left"], pid, rid, mask), [src], [], kind="rem")
        sent[0] += 2 * len(topo.engines(core, dst))

    from_prv = 2 * len(topo.engines(prv, core))
    from_nxt = 2 * len(topo.engines(nxt, core))

    def plane(b, a=0, e=C):
        return T.fh[:, C * b + a:C * b + e]

    def words(b, row, k):
        ts(T.al4[:, 10 * b:10 * b + 9], row, 4.0, float(b), (OP.mult, OP.add), [k], ["al4%d" % b])

    FL, FH, MT, XL, XH, G1, GL, XA = (["%s%d" % (s, b) for b in range(4)] for s in ("fl", "fh", "mt", "xl", "xh", "g1", "gl", "xa"))
    imprecise = {"allow_small_or_imprecise_dtypes": True}

    dma("s", T.bdi[:], T.bd[:], [], ["bdi"])
    dma("s", T.dsi[:], T.ds[:], [], ["dsi"])
    dma("s", T.xin[:], T.x[:], [], ["xin"])
    op("v", V.memset, (T.half[:], 0.5), [], ["half"])
    op("v", V.memset, (T.eb[:], 0.0), [], ["eb"])
    op("g", g.iota, (T.pidx[:], [[1, 1]], 0, 1), [], ["pidx"])
    op("g", g.iota, (T.jj16[:], [[0, 9], [1, 16]], 0, 0), [], ["jj16"], imprecise)
    op("g", g.affine_select, (T.eb[:, 3:515:4], T.half[:], [[-1, 128]], OP.is_equal, 0.0, 0, 1), ["half"], ["eb"])
    op("g", g.iota, (T.iof[:], [[1, C]], 0, 0), [], ["iof"], imprecise)
    op("g", g.iota, (T.jj4[:], [[0, 36], [1, 4]], 0, 0), [], ["jj4"], imprecise)
    dma("s", T.wq[:].bitcast(dt.uint8), T.wc[:], ["bdi"], ["wq"])
    dma("s", T.wsc[:], T.ws[:], [], ["wsc"])
    dma("s", T.uin[:], T.u[:], [], ["uin"])
    ts(T.pi3[:, 0:1], T.pidx[:], 15, None, (OP.bitwise_and,), ["pidx"], ["pi0"])
    ts(T.pi3[:, 1:2], T.pidx[:], 2, 3, (OP.logical_shift_right, OP.bitwise_and), ["pidx"], ["pi1"])
    ts(T.pi3[:, 2:3], T.pidx[:], 3, None, (OP.bitwise_and,), ["pidx"], ["pi2"])
    cp(T.pf[:, 0:3], T.pi3[:, 0:3], ["pi0", "pi1", "pi2"], ["pf"])
    ts(T.rb16[:, 0:K], T.jj16[:], 0.0, BIG, (OP.is_equal, OP.mult), ["jj16"], ["rb16"])
    ts(T.n16[:, 0:K], T.jj16[:], T.pf[:, 0:1], 2 * BIG, (OP.not_equal, OP.mult), ["jj16", "pf"], ["n16"])
    ts(T.pf[:, 3:4], T.pf[:, 2:3], float(C), None, (OP.mult,), ["pf"], ["pt"])
    ts(T.pf[:, 4:5], T.pf[:, 1:2], -2 * BIG, None, (OP.mult,), ["pf"], ["pn"])
    act(T.eb1[:], T.eb[:], ["eb"], ["eb1"], scale=2.0)
    act(T.rb16[:, K:C], T.rb16[:, 0:K], ["rb16"], ["rb16b"])
    act(T.phif[:, 0:K], T.iof[:, 0:K], ["iof"], ["phil"])
    act(T.phif[:, K:C], T.iof[:, K:C], ["iof"], ["phih"], FN.Identity, bias=float(K))
    act(T.n4[:, 0:K], T.jj4[:], ["jj4", "pn"], ["n4"], FN.Abs, bias=T.pf[:, 4:5], scale=2 * BIG)
    act(T.rb4[:, 0:K], T.jj4[:], ["jj4"], ["rb4"], FN.Relu, bias=BIG, scale=-BIG)
    for b in range(4):
        quant(T.qeh[:, 128 * b:128 * b + 128], T.seh[:, 128 * b:128 * b + 128], T.eb[:, 3 - b:515 - b], ["eb"], ["eh%d" % b])
    op("v", V.memset, (T.uoff[:, 0:1], 112), [], ["uo0"])
    cp(T.bdw[:], T.bdi[:], ["bdi"], ["bdw"])
    cp(T.ivrow[:].indirect(T.bdw[:]), T.iof[:], ["bdw", "iof"], ["tab0"])
    cp(T.dsw[:], T.dsi[:], ["dsi"], ["dsw"])
    tt(T.f1[:, 0:K], T.ivrow[:, K:C], T.n16[:, 0:K], OP.max, ["tab0", "n16"], ["f1"])
    act(T.urow[:], T.ivrow[:].indirect(T.dsw[:]), ["tab0", "dsw"], ["urow"])
    hold_scan(T.f2[:, 0:K], T.rb16[:, 0:K], T.f1[:, 0:K], ["rb16", "f1"], ["f2"])
    cp(T.aw[:, 0:9], T.f2[:, 15:K:16], ["f2"], ["aw0"])

    for r in range(R):
        aw, awk = T.aw[:, 10 * r:10 * r + 9], "aw%d" % r
        s0 = 432 * (r - 1)
        tabk = ["tab%d" % r] + (["tabh%d" % r] if r else [])
        low = T.sig[:, s0:s0 + K] if r else T.ivrow[:, 0:K]
        xw, xk = (T.xs[:], XL + XH) if r else (T.xin[:], ["xin"])

        if r:
            for b in range(4):
                act(T.g1[:, b:4 * K:4], plane(b).indirect(aw), [awk, FL[b], FH[b]], [G1[b]])
            cp(T.urow[:], T.sig[:, s0:s0 + 432].indirect(T.tw[:, 18 * (r - 1):18 * r]), tabk + ["tw%d" % r], ["urow"])
        else:
            for b in range(2):
                words(b, T.f2[:, 15:K:16], "f2")
        tt(T.e1[:], T.urow[:].indirect(aw), T.n4[:, 0:K], OP.max, ["urow", awk, "n4"], ["e1"])
        if r == 0:
            for b in range(2, 4):
                words(b, T.f2[:, 15:K:16], "f2")
            for b in range(4):
                act(T.g1[:, b:4 * K:4], xw.indirect(T.al4[:, 10 * b:10 * b + 9]), xk + ["al4%d" % b], [G1[b]])
        hold_scan(T.e2[:], T.rb4[:, 0:K], T.e1[:], ["rb4", "e1"], ["e2"])
        if r:
            ts(T.bw[:], T.e2[:, 3:K:4], T.pf[:, 3:4], None, (OP.add,), ["e2", "pt"], ["bw"])
            tt(T.mt[:], T.fh[:].indirect(T.bw[:]), T.g1[:], OP.add, ["bw"] + FL + FH + G1, MT)
        else:
            ts(T.bw[:], T.e2[:, 3:K:4], 4.0, T.pf[:, 2:3], (OP.mult, OP.add), ["e2", "pf"], ["bw"])
            xb = OPT["xb"]
            cp(T.xa[:, 0:16 * xb], xw.indirect(T.bw[:, 0:xb]), xk + ["bw"], XA[:2])
            act(T.xa[:, 16 * xb:4 * K], xw.indirect(T.bw[:, xb:36]), xk + ["bw"], XA[2:])
            quant(T.qa[:], T.sa[:], T.g1[:], G1, ["qa"])
            quant(T.qx[:, 0:K], T.sx[:, 0:K], T.xa[:], XA, ["qxl"])
            pair_sum(T.qa[:], T.sa[:], "qa", T.qx[:, 0:K], T.sx[:, 0:K], "qxl", T.mt, MT, True)
        quant(T["qm%d" % r][:], T["sqm%d" % r][:], T.mt[:], MT, ["qm%d" % r])
        send("qm", "lm", r, nxt, "am%d" % r)

        if r == 0:
            act(T.trow0[:], T.phif[:].indirect(T.dsw[:]), ["phil", "phih", "dsw"], ["trow0"])
        tt(T.f1[:, 0:K], low, T.n16[:, 0:K], OP.max, tabk[:1] + ["n16"], ["f1"])
        hold_scan(T.f2[:, 0:K], T.rb16[:, 0:K], T.f1[:, 0:K], ["rb16", "f1"], ["f2"])
        for b in range(4):
            words(b, T.f2[:, 15:K:16], "f2")
        alw, alk = T.alw[:, 10 * r:10 * r + 9], "alw%d" % r
        cp(alw, T.f2[:, 15:K:16], ["f2"], [alk])
        for b in range(4):
            (act if b < OPT["xa"] else cp)(T.xa[:, b:4 * K:4], xw.indirect(T.al4[:, 10 * b:10 * b + 9]), xk + ["al4%d" % b], [XA[b]])
        tt(T.e1[:], T.urow[:].indirect(alw), T.n4[:, 0:K], OP.max, ["urow", alk, "n4"], ["e1"])
        hold_scan(T.e2[:], T.rb4[:, 0:K], T.e1[:], ["rb4", "e1"], ["e2"])
        quant(T.qa[:], T.sa[:], T.xa[:], XA, ["qa"])
        halves(0, T.qa[:], T.sa[:], ["qa"], stop=False)
        if r == 1:
            ts(T.blw[:], T.e2[:, 3:K:4], T.pf[:, 3:4], None, (OP.add,), ["e2", "pt"], ["blw"])
            halves(4, T.qa[:], T.sa[:], ["qa"])
            for b in range(4):
                act(T.g1l[:, b:4 * K:4], bank(4 + b), ["ps%d" % (4 + b)], [GL[b]])
            act(T.trow1[:, 0:K], T.trow0[:].indirect(T.alw[:, 0:9]), ["trow0", "alw0"], ["trow1"])
            act(T.trow1[:, K:C], T.trow0[:].indirect(T.aw[:, 0:9]), ["trow0", "aw0"], ["trow1b"])
        else:
            ts(T.blw[:], T.e2[:, 3:K:4], 4.0, T.pf[:, 2:3], (OP.mult, OP.add), ["e2", "pf"], ["blw"])
        if r == 0:
            act(T.g1l[:], xw.indirect(T.blw[:]), xk + ["blw"], GL)
            for b in range(4):
                quant(T.qe1[:, 128 * b:128 * b + 128], T.se1[:, 128 * b:128 * b + 128], T.eb1[:, 3 - b:515 - b], ["eb1"], ["e1%d" % b])
            quant(T.qu[:], T.su[:], T.uin[:], ["uin"], ["qu"])
            ts(T.uoff[:, 1:8], T.iof[:, 0:7], 16.0, None, (OP.mult,), ["iof"], ["uo1"])
        if r == 2:
            act(T.sig[:, s0 + K:s0 + C], T.sig[:, s0 + C:s0 + 432], tabk + ["urow"], ["raw"])
            act(T.trow0[:, 0:K], T.sig[:, s0:s0 + C].indirect(T.alw[:, 10:19]), ["raw", "alw1"], ["trow0"])
            act(T.trow0[:, K:C], T.sig[:, s0:s0 + C].indirect(T.aw[:, 10:19]), ["raw", "aw1"], ["trow0b"])

        def targets(row, rowk, part):
            if part == 0:
                tt(T.h1[:, 0:K], row.indirect(alw), T.n16[:, 0:K], OP.max, rowk + [alk, "n16"], ["h1"])
                tt(T.h1[:, K:C], row.indirect(aw), T.n16[:, 0:K], OP.max, rowk + [awk, "n16"], ["h1b"])
            else:
                hold_scan(T.h2[:], T.rb16[:], T.h1[:], ["rb16", "rb16b", "h1", "h1b"], ["h2"])
                cp(T.tw[:, 18 * r:18 * r + 18], T.h2[:, 15:C:16], ["h2"], ["tw%d" % (r + 1)])

        halves(0, T["lm%d" % r][:], T["slm%d" % r][:], [], ext=[("am%d" % r, from_prv)], start=False)
        for b in range(4):
            (cp if b % 2 else act)(T.vt[:, b:4 * K:4], bank(b), ["ps%d" % b], ["vt%d" % b])
        quant(T.qw[:], T.sw[:], T.vt[:], ["vt%d" % b for b in range(4)], ["qw"])
        for b in range(4):
            mm(4 + b, T.wq, T.wsc, 128 * b, T.qw[:], T.sw[:], ["wq", "wsc", "qw"])
        for b in range(4):
            if b % 2 == 0:
                act(T.ht[:, b:4 * K:4], bank(4 + b), ["ps%d" % (4 + b)], ["ht%d" % b], scale=0.0078125)
            else:
                ts(T.ht[:, b:4 * K:4], bank(4 + b), 0.0078125, None, (OP.mult,), ["ps%d" % (4 + b)], ["ht%d" % b])
        quant(T["qh%d" % r][:], T["sqh%d" % r][:], T.ht[:], ["ht%d" % b for b in range(4)], ["qh%d" % r])
        send("qh", "lh", r, prv, "ah%d" % r)

        if r == 0:
            quant(T.qx[:, K:C], T.sx[:, K:C], T.g1l[:], GL, ["qxh"])
            pair_sum(T.qa[:], T.sa[:], "qa", T.qx[:, K:C], T.sx[:, K:C], "qxh", T.xs, XL, False)
            cp(T.qu2[:].bitcast(dt.uint32), T.qu[:].bitcast(dt.uint32).indirect(T.uoff[:]), ["qu", "uo0", "uo1"], ["qu2"])
            act(T.su2[:], T.su[:].indirect(T.uoff[:]), ["qu", "uo0", "uo1"], ["su2"])
            act(T.n16s[:], T.n16[:, 0:K], ["n16"], ["n16s"], FN.Identity, bias=-BIG)
            targets(T.trow0[:], ["trow0"], 0)
        if r == 1:
            tt(T.xs[:, 0:4 * K], T.fh[:].indirect(T.blw[:]), T.g1l[:], OP.add, ["blw"] + FL + FH + GL, XL)
            act(T.sig[:, 432:432 + C], T.iof[:], ["iof"], ["tab2"])
            act(T.sig[:, 864:864 + C], T.iof[:], ["iof"], ["tab3"])
            act(T.n16[:, K:C], T.n16[:, 0:K], ["n16"], ["n16b"])
            act(T.n4[:, K:C], T.n4[:, 0:K], ["n4"], ["n4b"])
            act(T.rb4[:, K:C], T.rb4[:, 0:K], ["rb4"], ["rb4b"])
        if r < R - 1:
            quant(T.qx[:, 0:K], T.sx[:, 0:K], T.xs[:, 0:4 * K], XL, ["qxl"])
            halves(0, T.qx[:, 0:K], T.sx[:, 0:K], ["qxl"])
            for b in range(4):
                act(plane(b, 0, K), bank(b), ["ps%d" % b], [FL[b]])
        if r == 0:
            targets(T.trow0[:], ["trow0"], 1)
            act(T.rs16[:], T.jj16[:], ["jj16"], ["rs16"], FN.Sign)
            act(T.kw[:], T.iof[:, K:C:16], ["iof", "pf"], ["kw0"], FN.Identity, bias=T.pf[:, 0:1])
            act(T.sig[:, 0:C], T.iof[:], ["iof"], ["tab1"])
            ts(T.kw[:], T.kw[:], 16.0, None, (OP.add,), ["kw0"], ["kw"])
        elif r == 1:
            targets(T.trow1[:], ["trow1", "trow1b"], 0)
            targets(T.trow1[:], ["trow1", "trow1b"], 1)
            quant(T.qv[:], T.sv[:], T.vin[:], ["vin"], ["qv"])
        else:
            act(T.g1l[:], xw.indirect(T.blw[:]), xk + ["blw"], GL)
            tt(T.h1[:], T.trow0[:].indirect(T.bdw[:]), T.n4[:], OP.max, ["trow0", "trow0b", "bdw", "n4", "n4b"], ["h1", "h1b"])
            hold_scan(T.h2[:], T.rb4[:], T.h1[:], ["rb4", "rb4b", "h1", "h1b"], ["h2"])
            ts(T.xw[:], T.h2[:, 3:C:4], 4.0, T.pf[:, 2:3], (OP.mult, OP.add), ["h2", "pf"], ["xw"])
            quant(T.qx[:, 0:K], T.sx[:, 0:K], T.g1l[:], GL, ["qxl"])
            pair_sum(T.qa[:], T.sa[:], "qa", T.qx[:, 0:K], T.sx[:, 0:K], "qxl", T.xs, XL, False)
            tt(T.f1[:], T.trow0[:].indirect(T.bdw[:]), T.n16[:], OP.max, ["trow0", "trow0b", "bdw", "n16", "n16b"], ["f1"])
            hold_scan(T.f2[:], T.rb16[:], T.f1[:], ["rb16", "rb16b", "f1"], ["f2"])
            ts(T.k1[:], T.f2[:, 15:C:16], float(K), float(K), (OP.is_ge, OP.mult), ["f2"], ["k1"])
            tt(T.k2[:], T.f2[:, 15:C:16], T.k1[:], OP.add, ["f2", "k1"], ["k2"])
            cp(T.pw[:], T.k2[:], ["k2"], ["pw2"])

        lh, slh = T["lh%d" % r][:], T["slh%d" % r][:]
        na, ns, fpos, qpos = OPT["na"][r], OPT["ns"][r], OPT["fpos"][r], OPT["qpos"][r]
        mm(0, T.qu2, T.su2, 0, lh, slh, ["qu2", "su2"], ext=[("ah%d" % r, from_nxt)])
        for b in range(4):
            if b == 2 and ns:
                mm(1, T.qu2, T.su2, 0, lh, slh, ["qu2", "su2"])
            mm(4 + b, T.qe1, T.se1, 128 * b, lh, slh, ["e1%d" % b])

        def add(b):
            tt(T.xs[:, 4 * K + b:4 * C:4], bank(4 + b), T.mt[:, b:4 * K:4], OP.add, ["ps%d" % (4 + b), MT[b]], [XH[b]])

        def state():
            if r < R - 1:
                quant(T.qx[:, K:C], T.sx[:, K:C], T.xs[:, 4 * K:4 * C], XH, ["qxh"])
                halves(4, T.qx[:, K:C], T.sx[:, K:C], ["qxh"])
            elif OPT["xv"]:
                cp(T.xf[:, 0:16 * OPT["xv"]], T.xs[:].indirect(T.xw[:, 0:OPT["xv"]]), XL + XH + ["xw"], ["xfv"])

        def unload():
            if r < R - 1:
                for b in range(4):
                    act(plane(b, K, C), bank(4 + b), ["ps%d" % (4 + b)], [FH[b]])
            else:
                xv = OPT["xv"]
                act(T.xf[:, 16 * xv:4 * C], T.xs[:].indirect(T.xw[:, xv:72]), XL + XH + ["xw"], ["xf"])

        def compare(c):
            e = 16 * c + 16
            s = T.hold[:, e - 1:e]
            ts(T.cmp[:, CW * c:CW * c + e], bank(0, 0, e), s, None, (OP.is_le,), ["ps0", "hold"], ["ca%d" % c])
            if e < K and c >= ns:
                ts(T.cmp[:, CW * c + e:CW * c + K], bank(0, e, K), s, None, (OP.is_lt,), ["ps0", "hold"], ["cb%d" % c])

        def total(c):
            reg, keys = T.cmp[:, CW * c:CW * c + K + 1], ["ca%d" % c, "cb%d" % c]
            if c < na:
                act(reg, reg, keys + ["pen"], keys + ["cnt%d" % c, "pen%d" % c], FN.Relu, accum_out=T.cnt[:, c:c + 1])
            else:
                op("v", V.tensor_reduce, (T.cnt[:, c:c + 1], reg, AxisListType.X, OP.add), keys + ["pen"], ["cnt%d" % c])

        late = OPT["late"][r]
        tt(T.d1[:], bank(0), T.n16s[:], OP.max, ["ps0", "n16s"], ["d1"])
        if r == 0:
            dma("s", T.vin[:], T.v[:], ["d1"], ["vin"])
        for b in range(4 if late < 0 else 1):
            add(b)
        if late < 0:
            unload()
        hold_scan(T.hold[:], T.rb16[:, 0:K], T.d1[:], ["rb16", "d1"], ["hold"])
        for c in range(ns):
            e = 16 * c + 16
            act(T.cmp[:, CW * c + e:CW * c + K], bank(1, e, K), ["ps1", "hold"], ["cb%d" % c], FN.Sign, bias=T.hold[:, e - 1:e], scale=-1.0)
        if late >= 0:
            add(1)
        tt(T.eq[:], bank(0), T.hold[:], OP.not_equal, ["ps0", "hold"], ["eq"])
        if not late:
            add(2)
        ts(T.flag[:], T.hold[:, 15:K:16], 0.0, 512.0, (OP.is_gt, OP.mult), ["hold"], ["flag"])
        op("v", V.tensor_tensor_scan, (T.eqs[:], T.rs16[:], T.eq[:], 0.0, OP.mult, OP.add), ["rs16", "eq"], ["eqs"])
        if not late:
            add(3)
        compare(0)
        tt(T.cmp[:, K:9 * CW:CW], T.flag[:], T.eqs[:, 15:K:16], OP.add, ["flag", "eqs"], ["pen"] + ["pen%d" % c for c in range(9)])
        for c in range(1, 9):
            if c == late:
                add(2)
                add(3)
            if c == qpos:
                state()
            compare(c)
        for c in range(fpos):
            total(c)
        if late >= 0:
            unload()
        if r == R - 1:
            quant(T.qf[:], T.sf[:], T.xf[:], ["xf", "xfv"], ["qf"])
            dma("s", T.oc[:], T.qf[:].bitcast(dt.uint8), ["qf"], [])
            for h in range(2):
                mm(2 + h, T.qv, T.sv, 0, T.qf[:, K * h:K * h + K], T.sf[:, K * h:K * h + K], ["qv", "qf"])
        for c in range(fpos, 9):
            if r == R - 1 and c == OPT["ypos"]:
                for h in range(2):
                    act(T.yb[:, K * h:K * h + K], bank(2 + h), ["ps%d" % (2 + h)], ["yb%d" % h])
                dma("a", T.y[:], T.yb[:], ["yb0", "yb1"], [])
            total(c)
        if r == R - 1:
            for k in range(4):
                dma("s", T.osc[4 * k:4 * k + 4, :], T.sf[32 * k:32 * k + 4, :], ["qf"], [])
        tt(T.af[:], T.cnt[:], T.kw[:], OP.min, ["cnt%d" % c for c in range(9)] + ["kw"], ["af"])
        aw, awk = T.aw[:, 10 * r + 10:10 * r + 19], "aw%d" % (r + 1)
        ts(aw, T.af[:], -16.0, None, (OP.add,), ["af"], [awk])
        s1 = 432 * r
        act(T.sig[:, s1 + C:s1 + 432], T.iof[:].indirect(aw), [awk, "iof"], ["tabh%d" % (r + 1)])
        cp(T.sig[:, s1:s1 + C].indirect(aw), T.iof[:, K:C], [awk, "iof"], ["tab%d" % (r + 1)])

    cp(T.obr[:, 0:160], T.sig[:, 864:1296].indirect(T.pw[:, 0:10]), ["tab3", "tabh3", "pw2"], ["ob0"])
    act(T.obr[:, 160:C], T.sig[:, 864:1296].indirect(T.pw[:, 10:18]), ["tab3", "tabh3", "pw2"], ["ob1"])
    dma("s", T.ob[:], T.obr[0:128:16, :], ["ob0", "ob1"], [])

    emit(ops, queues, T)
    g.wait_ge(T.sem["left"], sent[0])
